import numpy as np
import ml_dtypes


def mxq(x, axis, fmt="e4m3"):
    dtype, down = {"e4m3": (ml_dtypes.float8_e4m3fn, 7), "e5m2": (ml_dtypes.float8_e5m2, 14)}[fmt]
    v = np.moveaxis(np.asarray(x, np.float32).astype(ml_dtypes.bfloat16).astype(np.float64), axis, -1)
    blocks = v.reshape(v.shape[:-1] + (-1, 32))
    amax = np.abs(blocks).max(-1, keepdims=True)
    byte = np.maximum(np.where(amax > 0, np.frexp(amax)[1] - 1 + 127, 0) - down, 1)
    scale = np.exp2(byte - 127.0)
    codes = (blocks / scale).astype(np.float32).astype(dtype).astype(np.float64)
    return np.moveaxis((codes * scale).reshape(v.shape), -1, axis)


WIDE = False


def mx_kscale(k):
    if not WIDE:
        return np.ones(k)
    levels = np.array([10, -10, 5, -5, 0])
    if k % 512:
        return np.exp2(np.random.permutation(np.resize(levels, k // 32))).repeat(32)
    a = np.empty((k // 512, 16))
    for p in range(k // 512):
        a[p, :8] = np.random.permutation(np.resize(levels, 8))
        for g in range(8):
            far = levels[np.abs(levels - a[p, g]) >= 10]
            a[p, g + 8] = far[np.random.randint(len(far))]
    return np.exp2(a.ravel()).repeat(32)


def f64(x):
    return np.asarray(x).astype(np.float64)


def striped(idx):
    return np.tile(np.asarray(idx).reshape(-1, 16).T, (8, 1)).astype(np.uint16)


def unstriped(offs):
    return offs[:16].T.reshape(-1).astype(np.int64)


E2M1 = np.array([0.0, 0.5, 1.0, 1.5, 2.0, 3.0, 4.0, 6.0, -0.0, -0.5, -1.0, -1.5, -2.0, -3.0, -4.0, -6.0])


def pack_weight(w, fmt):
    k, n = w.shape
    w = f64(np.asarray(w, np.float32).astype(ml_dtypes.bfloat16)).reshape(k // 32, 32, n)
    amax = np.abs(w).max(1)
    if fmt == "e4m3":
        byte = np.frexp(amax)[1] - 1 + 127 - 7
    else:
        mant, ex = np.frexp(amax / 6.0)
        byte = np.where(mant > 0.5, ex, ex - 1) + 127
    byte = np.clip(np.where(amax > 0, byte, 1), 1, 254)
    scaled = (w * np.exp2(127.0 - byte)[:, None, :]).reshape(k, n).astype(np.float32)
    by_word = np.ascontiguousarray(scaled.reshape(k // 512, 128, 4, n).transpose(0, 1, 3, 2))
    if fmt == "e4m3":
        words = by_word.astype(ml_dtypes.float8_e4m3fn).view(np.uint8)
    else:
        c = by_word.astype(ml_dtypes.float4_e2m1fn).view(np.uint8) & 0xF
        words = (c[..., 0::2] | (c[..., 1::2] << 4)).reshape(k // 512, 128, 2 * n)
    return np.ascontiguousarray(words), np.ascontiguousarray(byte.astype(np.uint8).reshape(k // 512, 16, n))


def unpack_weight(words, scales, fmt):
    g, _, n = scales.shape
    words = np.ascontiguousarray(words).reshape(g, 128, n, -1)
    if fmt == "e4m3":
        vals = words.view(ml_dtypes.float8_e4m3fn).astype(np.float64)
    else:
        nib = np.empty((g, 128, n, 4), np.uint8)
        nib[..., 0::2] = words & 0xF
        nib[..., 1::2] = words >> 4
        vals = E2M1[nib]
    vals = vals * np.repeat(np.exp2(scales.astype(np.float64) - 127.0), 8, axis=1)[..., None]
    return vals.transpose(0, 1, 3, 2).reshape(g * 512, n)


D, T, I, J, U, Z, E = 512, 2048, 512, 512, 1024, 1024, 512


def setup_inputs():
    n = np.random.standard_normal
    idx = np.random.permutation(T)[:I]
    idx2 = np.random.permutation(U)[:J]
    idx3 = np.random.permutation(Z)[:J]
    fd = mx_kscale(D)
    fi = mx_kscale(I)
    ti = np.ones(T)
    ti[idx] = fi
    keysp = pack_weight(n((D, T)) / fd[:, None], "e4m3")
    return {
        "keys_words": keysp[0],
        "keys_scales": keysp[1],
        "notes": (n((D, U)) * 1.0 / np.sqrt(D) * fd[:, None]).astype(np.float32),
        "given": (np.random.uniform(0.3, 1.7, (I, Z))).astype(np.float32),
        "rowf": (np.random.uniform(0.02, 0.08, (I, 1)) * fi[:, None]).astype(np.float32),
        "vals": (n((E, T)) / ti).astype(np.float32),
        "offs": striped(idx),
        "offs2": striped(idx2),
        "offs3": striped(idx3),
    }


def reference(keys_words, keys_scales, notes, given, rowf, vals, offs, offs2, offs3):
    idx = unstriped(offs)
    idx2 = unstriped(offs2)
    idx3 = unstriped(offs3)
    keysu = unpack_weight(keys_words, keys_scales, "e4m3")
    keysidxg = keysu[:, idx]
    notesidx2q = mxq(f64(notes)[:, idx2], 0, "e4m3")
    g1 = keysidxg.T @ notesidx2q
    g0 = g1 * f64(given)[:, idx3]
    gr1 = g0 * f64(rowf)
    vt1 = f64(vals)[:, idx].T
    vt1q = mxq(vt1, 0, "e4m3")
    gr1q = mxq(gr1, 0, "e4m3")
    o = vt1q.T @ gr1q
    return o

@@ -1,0 +1,178 @@
+from contextlib import ExitStack
+
+import concourse.mybir as mybir
+from concourse.masks import make_identity
+
+D, T, I, J, U, Z, E = 512, 2048, 512, 512, 1024, 1024, 512
+FLOPS = 2 * D * I * J + 2 * I * E * J
+
+F32 = mybir.dt.float32
+BF16 = mybir.dt.bfloat16
+I32 = mybir.dt.int32
+U32 = mybir.dt.uint32
+U16 = mybir.dt.uint16
+U8 = mybir.dt.uint8
+FP8X4 = mybir.dt.float8_e4m3fn_x4
+MULT = mybir.AluOpType.mult
+COPY = mybir.ActivationFunctionType.Copy
+
+P = 128
+PACK = 4
+LIST_COLS = 32
+HALF = 256
+
+
+def interleave(nc, woven, planes):
+    nc.vector.tensor_copy(
+        out=woven[:].rearrange("p (c i) t -> p c t i", i=4),
+        in_=planes[:].rearrange("p t (c i) -> p c t i", i=4),
+    )
+
+
+def tile_attend_tab_timestable_exchange_kernel(
+    tc, keys_words, keys_scales, notes, given, rowf, vals, offs, offs2, offs3, out
+):
+    nc = tc.nc
+    with ExitStack() as ctx:
+        keep = ctx.enter_context(tc.tile_pool(name="keep", bufs=1))
+        ring = ctx.enter_context(tc.tile_pool(name="ring", bufs=2))
+        psum = ctx.enter_context(tc.psum_pool(name="psum", bufs=1))
+
+        token_list = keep.tile([P, LIST_COLS], U16, name="token_list")
+        note_list = keep.tile([P, LIST_COLS], U16, name="note_list")
+        given_list = keep.tile([P, LIST_COLS], U16, name="given_list")
+        key_words = keep.tile([P, T], U32, name="key_words")
+        key_bytes = keep.tile([P, T], U8, name="key_bytes")
+        row_factor = keep.tile([P, PACK], F32, name="row_factor")
+        note_pool = [keep.tile([P, U], F32, name="note_pool%d" % t) for t in range(PACK)]
+        given_pool = [keep.tile([P, Z], F32, name="given_pool%d" % t) for t in range(PACK)]
+        val_pool = [keep.tile([P, T], F32, name="val_pool%d" % b) for b in range(E // P)]
+        identity = keep.tile([P, P], F32, name="identity")
+
+        notes_by_place = notes.rearrange("(p t) u -> t p u", t=PACK)
+        given_by_place = given.rearrange("(p t) z -> t p z", t=PACK)
+
+        nc.gpsimd.memset(key_bytes[:].bitcast(I32), 0)
+        for t in range(3):
+            nc.sync.dma_start(note_pool[t][:], notes_by_place[t])
+        for q in range(4):
+            nc.sync.dma_start(
+                key_bytes[32 * q : 32 * q + 4, :].bitcast(I32),
+                keys_scales[0, 4 * q : 4 * q + 4, :].bitcast(I32),
+            )
+        nc.sync.dma_start(note_list[:], offs2)
+        nc.sync.dma_start(note_pool[3][:], notes_by_place[3])
+        nc.sync.dma_start(
+            key_words[:].bitcast(I32),
+            keys_words[0].rearrange("p n t -> p (n t)").bitcast(I32),
+        )
+        nc.sync.dma_start(token_list[:], offs)
+        nc.sync.dma_start(given_list[:], offs3)
+        nc.sync.dma_start(row_factor[:], rowf.rearrange("(p t) o -> p (t o)", t=PACK))
+        for t in range(PACK):
+            nc.sync.dma_start(given_pool[t][:], given_by_place[t])
+        for b in range(E // P):
+            nc.sync.dma_start(val_pool[b][:], vals[b * P : (b + 1) * P, :])
+        make_identity(nc, identity[:])
+
+        note_planes = keep.tile([P, PACK, J], BF16, name="note_planes")
+        for t in range(PACK):
+            picked = note_pool[t][:].indirect(note_list[:])
+            if t % 2 == 0:
+                nc.scalar.activation(note_planes[:, t, :], picked, COPY)
+            else:
+                nc.vector.tensor_copy(note_planes[:, t, :], picked)
+
+        key_codes = keep.tile([P, PACK, P], U32, name="key_codes", align_bytes=64)
+        key_scales = keep.tile([P, PACK, P], U8, name="key_scales", align_bytes=64)
+        nc.vector.tensor_copy(
+            key_scales[:].rearrange("p t m -> p m t"), key_bytes[:].indirect(token_list[:])
+        )
+
+        note_woven = keep.tile([P, J, PACK], BF16, name="note_woven", align_bytes=64)
+        interleave(nc, note_woven, note_planes)
+        nc.vector.tensor_copy(
+            key_codes[:].rearrange("p t m -> p m t"), key_words[:].indirect(token_list[:])
+        )
+        note_codes = keep.tile([P, J], U32, name="note_codes", align_bytes=64)
+        note_scales = keep.tile([P, J], U8, name="note_scales", align_bytes=64)
+        nc.vector.quantize_mx(
+            out=note_codes[:].bitcast(FP8X4),
+            scales=note_scales[:],
+            in_=note_woven[:].rearrange("p j t -> p (j t)"),
+        )
+
+        table_planes = keep.tile([P, PACK, J], BF16, name="table_planes")
+        for t in range(PACK):
+            given_picked = keep.tile([P, J], F32, name="given_picked%d" % t)
+            nc.scalar.activation(given_picked[:], given_pool[t][:].indirect(given_list[:]), COPY)
+            products = psum.tile([P, J], F32, name="products", tag="acc", bufs=6)
+            nc.tensor.matmul_mx(
+                out=products[:],
+                lhsT=key_codes[:, t, :].bitcast(FP8X4),
+                lhsT_scale=key_scales[:, t, :],
+                rhs=note_codes[:].bitcast(FP8X4),
+                rhs_scale=note_scales[:],
+                start=True,
+                stop=True,
+            )
+            nc.vector.scalar_tensor_tensor(
+                out=table_planes[:, t, :],
+                in0=products[:],
+                scalar=row_factor[:, t : t + 1],
+                in1=given_picked[:],
+                op0=MULT,
+                op1=MULT,
+            )
+        table_woven = keep.tile([P, J, PACK], BF16, name="table_woven", align_bytes=64)
+        interleave(nc, table_woven, table_planes)
+        table_codes = keep.tile([P, J], U32, name="table_codes", align_bytes=64)
+        table_scales = keep.tile([P, J], U8, name="table_scales", align_bytes=64)
+        nc.vector.quantize_mx(
+            out=table_codes[:].bitcast(FP8X4),
+            scales=table_scales[:],
+            in_=table_woven[:].rearrange("p j t -> p (j t)"),
+        )
+
+        for b in range(E // P):
+            val_picked = ring.tile([P, I], BF16, name="val_picked")
+            nc.vector.tensor_copy(
+                val_picked[:, 0:HALF], val_pool[b][:].indirect(token_list[:, 0:16])
+            )
+            nc.scalar.activation(
+                val_picked[:, HALF:I], val_pool[b][:].indirect(token_list[:, 16:32]), COPY
+            )
+            pairs = val_picked[:].bitcast(F32)
+            turned = psum.tile([P, 2, P], F32, name="turned", tag="turned", bufs=2)
+            for u in range(2):
+                nc.tensor.transpose(turned[:, u, :], pairs[:, u : 2 * P : 2], identity[:])
+            val_woven = keep.tile([P, P, PACK], BF16, name="val_woven%d" % b, align_bytes=64)
+            nc.scalar.copy(
+                val_woven[:].rearrange("p e t -> p (e t)").bitcast(F32).rearrange("p (e u) -> p e u", u=2),
+                turned[:].rearrange("p u e -> p e u"),
+            )
+            val_codes = keep.tile([P, P], U32, name="val_codes%d" % b, align_bytes=64)
+            val_scales = keep.tile([P, P], U8, name="val_scales%d" % b, align_bytes=64)
+            nc.vector.quantize_mx(
+                out=val_codes[:].bitcast(FP8X4),
+                scales=val_scales[:],
+                in_=val_woven[:].rearrange("p e t -> p (e t)"),
+            )
+            result = keep.tile([P, J], F32, name="result%d" % b)
+            for h in range(2):
+                cols = slice(h * HALF, (h + 1) * HALF)
+                sums = psum.tile([P, HALF], F32, name="sums", tag="acc", bufs=6)
+                nc.tensor.matmul_mx(
+                    out=sums[:],
+                    lhsT=val_codes[:].bitcast(FP8X4),
+                    lhsT_scale=val_scales[:],
+                    rhs=table_codes[:, cols].bitcast(FP8X4),
+                    rhs_scale=table_scales[:, cols],
+                    start=True,
+                    stop=True,
+                )
+                if h == 0:
+                    nc.scalar.copy(result[:, cols], sums[:])
+                else:
+                    nc.vector.tensor_copy(result[:, cols], sums[:])
+            nc.sync.dma_start(out[b * P : (b + 1) * P, :], result[:])

@@ -20,6 +20,7 @@ P = 128
 PACK = 4
 LIST_COLS = 32
 HALF = 256
+SHARE = 176
 
 
 def interleave(nc, woven, planes):
@@ -35,7 +36,6 @@ def tile_attend_tab_timestable_exchange_kernel(
     nc = tc.nc
     with ExitStack() as ctx:
         keep = ctx.enter_context(tc.tile_pool(name="keep", bufs=1))
-        ring = ctx.enter_context(tc.tile_pool(name="ring", bufs=2))
         psum = ctx.enter_context(tc.psum_pool(name="psum", bufs=1))
 
         token_list = keep.tile([P, LIST_COLS], U16, name="token_list")
@@ -46,51 +46,58 @@ def tile_attend_tab_timestable_exchange_kernel(
         row_factor = keep.tile([P, PACK], F32, name="row_factor")
         note_pool = [keep.tile([P, U], F32, name="note_pool%d" % t) for t in range(PACK)]
         given_pool = [keep.tile([P, Z], F32, name="given_pool%d" % t) for t in range(PACK)]
-        val_pool = [keep.tile([P, T], F32, name="val_pool%d" % b) for b in range(E // P)]
+        val_pool = [
+            keep.tile([P, T], F32, name="val_pool%d" % b, tag="val_pool%d" % b, align_bytes=64)
+            for b in range(E // P)
+        ]
         identity = keep.tile([P, P], F32, name="identity")
 
         notes_by_place = notes.rearrange("(p t) u -> t p u", t=PACK)
         given_by_place = given.rearrange("(p t) z -> t p z", t=PACK)
 
-        nc.gpsimd.memset(key_bytes[:].bitcast(I32), 0)
-        for t in range(3):
-            nc.sync.dma_start(note_pool[t][:], notes_by_place[t])
-        for q in range(4):
-            nc.sync.dma_start(
-                key_bytes[32 * q : 32 * q + 4, :].bitcast(I32),
-                keys_scales[0, 4 * q : 4 * q + 4, :].bitcast(I32),
-            )
+        byte_rows = keep.tile([P, T // 4], I32, name="byte_rows")
+        nc.sync.dma_start(note_pool[0][:], notes_by_place[0])
         nc.sync.dma_start(note_list[:], offs2)
+        for r in range(4):
+            nc.sync.dma_start(byte_rows[r:P:32, :], keys_scales[0, r:16:4, :].bitcast(I32))
+        for t in range(1, 3):
+            nc.sync.dma_start(note_pool[t][:], notes_by_place[t])
+        nc.sync.dma_start(token_list[:], offs)
         nc.sync.dma_start(note_pool[3][:], notes_by_place[3])
         nc.sync.dma_start(
             key_words[:].bitcast(I32),
             keys_words[0].rearrange("p n t -> p (n t)").bitcast(I32),
         )
-        nc.sync.dma_start(token_list[:], offs)
         nc.sync.dma_start(given_list[:], offs3)
+        nc.sync.dma_start(given_pool[0][:], given_by_place[0])
         nc.sync.dma_start(row_factor[:], rowf.rearrange("(p t) o -> p (t o)", t=PACK))
-        for t in range(PACK):
+        for t in range(1, PACK):
             nc.sync.dma_start(given_pool[t][:], given_by_place[t])
         for b in range(E // P):
             nc.sync.dma_start(val_pool[b][:], vals[b * P : (b + 1) * P, :])
+        nc.vector.memset(key_bytes[:].bitcast(I32), 0)
+        for q in range(4):
+            nc.vector.tensor_copy(
+                key_bytes[32 * q : 32 * q + 4, :].bitcast(I32), byte_rows[32 * q : 32 * q + 4, :]
+            )
         make_identity(nc, identity[:])
 
-        note_planes = keep.tile([P, PACK, J], BF16, name="note_planes")
+        note_planes = keep.tile([P, PACK, J], BF16, name="note_planes", tag="note_planes", align_bytes=64)
+        key_scales = keep.tile([P, PACK, P], U8, name="key_scales", align_bytes=64)
         for t in range(PACK):
             picked = note_pool[t][:].indirect(note_list[:])
             if t % 2 == 0:
                 nc.scalar.activation(note_planes[:, t, :], picked, COPY)
             else:
                 nc.vector.tensor_copy(note_planes[:, t, :], picked)
+            if t == 1:
+                nc.vector.tensor_copy(
+                    key_scales[:].rearrange("p t m -> p m t"), key_bytes[:].indirect(token_list[:])
+                )
 
-        key_codes = keep.tile([P, PACK, P], U32, name="key_codes", align_bytes=64)
-        key_scales = keep.tile([P, PACK, P], U8, name="key_scales", align_bytes=64)
-        nc.vector.tensor_copy(
-            key_scales[:].rearrange("p t m -> p m t"), key_bytes[:].indirect(token_list[:])
-        )
-
-        note_woven = keep.tile([P, J, PACK], BF16, name="note_woven", align_bytes=64)
+        note_woven = keep.tile([P, J, PACK], BF16, name="note_woven", tag="odd_given", align_bytes=64)
         interleave(nc, note_woven, note_planes)
+        key_codes = keep.tile([P, PACK, P], U32, name="key_codes", tag="note_planes", align_bytes=64)
         nc.vector.tensor_copy(
             key_codes[:].rearrange("p t m -> p m t"), key_words[:].indirect(token_list[:])
         )
@@ -102,10 +109,14 @@ def tile_attend_tab_timestable_exchange_kernel(
             in_=note_woven[:].rearrange("p j t -> p (j t)"),
         )
 
-        table_planes = keep.tile([P, PACK, J], BF16, name="table_planes")
+        table_planes = keep.tile([P, PACK, J], BF16, name="table_planes", tag="table_planes", align_bytes=64)
         for t in range(PACK):
-            given_picked = keep.tile([P, J], F32, name="given_picked%d" % t)
-            nc.scalar.activation(given_picked[:], given_pool[t][:].indirect(given_list[:]), COPY)
+            given_picked = keep.tile(
+                [P, J], F32, name="given_picked%d" % t,
+                tag="given_picked%d" % t, align_bytes=64,
+            )
+            picked = given_pool[t][:].indirect(given_list[:])
+            nc.scalar.activation(given_picked[:], picked, COPY)
             products = psum.tile([P, J], F32, name="products", tag="acc", bufs=6)
             nc.tensor.matmul_mx(
                 out=products[:],
@@ -124,8 +135,15 @@ def tile_attend_tab_timestable_exchange_kernel(
                 op0=MULT,
                 op1=MULT,
             )
-        table_woven = keep.tile([P, J, PACK], BF16, name="table_woven", align_bytes=64)
-        interleave(nc, table_woven, table_planes)
+        table_woven = keep.tile([P, J, PACK], BF16, name="table_woven", tag="table_woven", align_bytes=64)
+        nc.scalar.copy(
+            table_woven[:, 0:SHARE, :].rearrange("p (c i) t -> p c t i", i=4),
+            table_planes[:, :, 0:SHARE].rearrange("p t (c i) -> p c t i", i=4),
+        )
+        nc.vector.tensor_copy(
+            table_woven[:, SHARE:J, :].rearrange("p (c i) t -> p c t i", i=4),
+            table_planes[:, :, SHARE:J].rearrange("p t (c i) -> p c t i", i=4),
+        )
         table_codes = keep.tile([P, J], U32, name="table_codes", align_bytes=64)
         table_scales = keep.tile([P, J], U8, name="table_scales", align_bytes=64)
         nc.vector.quantize_mx(
@@ -134,8 +152,11 @@ def tile_attend_tab_timestable_exchange_kernel(
             in_=table_woven[:].rearrange("p j t -> p (j t)"),
         )
 
-        for b in range(E // P):
-            val_picked = ring.tile([P, I], BF16, name="val_picked")
+        blocks = E // P
+
+        def gather_and_turn(b):
+            tenant_of = ["given_picked3", "table_planes", "val_picked2", "val_picked3"][b]
+            val_picked = keep.tile([P, I], BF16, name="val_picked%d" % b, tag=tenant_of, align_bytes=64)
             nc.vector.tensor_copy(
                 val_picked[:, 0:HALF], val_pool[b][:].indirect(token_list[:, 0:16])
             )
@@ -146,7 +167,12 @@ def tile_attend_tab_timestable_exchange_kernel(
             turned = psum.tile([P, 2, P], F32, name="turned", tag="turned", bufs=2)
             for u in range(2):
                 nc.tensor.transpose(turned[:, u, :], pairs[:, u : 2 * P : 2], identity[:])
-            val_woven = keep.tile([P, P, PACK], BF16, name="val_woven%d" % b, align_bytes=64)
+            return turned
+
+        def multiply(b, turned):
+            val_woven = keep.tile(
+                [P, P, PACK], BF16, name="val_woven%d" % b, tag="val_pool%d" % (b + 1), align_bytes=64
+            )
             nc.scalar.copy(
                 val_woven[:].rearrange("p e t -> p (e t)").bitcast(F32).rearrange("p (e u) -> p e u", u=2),
                 turned[:].rearrange("p u e -> p e u"),
@@ -158,10 +184,20 @@ def tile_attend_tab_timestable_exchange_kernel(
                 scales=val_scales[:],
                 in_=val_woven[:].rearrange("p e t -> p (e t)"),
             )
-            result = keep.tile([P, J], F32, name="result%d" % b)
-            for h in range(2):
-                cols = slice(h * HALF, (h + 1) * HALF)
-                sums = psum.tile([P, HALF], F32, name="sums", tag="acc", bufs=6)
+            return val_codes, val_scales
+
+        def finish(b, val_codes, val_scales):
+            result = keep.tile([P, J], F32, name="result%d" % b, tag=("val_pool%d" % (b + 2)) if b < 2 else "result%d" % b, align_bytes=64)
+            copy_out = [
+                [nc.vector.tensor_copy],
+                [nc.vector.tensor_copy],
+                [nc.scalar.copy],
+                [nc.scalar.copy, nc.vector.tensor_copy],
+            ][b]
+            width = J // len(copy_out)
+            for h, copy in enumerate(copy_out):
+                cols = slice(h * width, (h + 1) * width)
+                sums = psum.tile([P, width], F32, name="sums", tag="acc", bufs=6)
                 nc.tensor.matmul_mx(
                     out=sums[:],
                     lhsT=val_codes[:].bitcast(FP8X4),
@@ -171,8 +207,15 @@ def tile_attend_tab_timestable_exchange_kernel(
                     start=True,
                     stop=True,
                 )
-                if h == 0:
-                    nc.scalar.copy(result[:, cols], sums[:])
-                else:
-                    nc.vector.tensor_copy(result[:, cols], sums[:])
+                copy(result[:, cols], sums[:])
             nc.sync.dma_start(out[b * P : (b + 1) * P, :], result[:])
+
+        turned_blocks = []
+        operands = []
+        for step in range(blocks + 2):
+            if step < blocks:
+                turned_blocks.append(gather_and_turn(step))
+            if 1 <= step <= blocks:
+                operands.append(multiply(step - 1, turned_blocks[step - 1]))
+            if step >= 2:
+                finish(step - 2, *operands[step - 2])

@@ -21,6 +21,8 @@ PACK = 4
 LIST_COLS = 32
 HALF = 256
 SHARE = 176
+POOL_BYTES = 4 * T
+WOVEN_BYTES = 2 * PACK * P
 
 
 def interleave(nc, woven, planes):
@@ -36,6 +38,7 @@ def tile_attend_tab_timestable_exchange_kernel(
     nc = tc.nc
     with ExitStack() as ctx:
         keep = ctx.enter_context(tc.tile_pool(name="keep", bufs=1))
+        values = ctx.enter_context(tc.tile_pool(name="values", bufs=1))
         psum = ctx.enter_context(tc.psum_pool(name="psum", bufs=1))
 
         token_list = keep.tile([P, LIST_COLS], U16, name="token_list")
@@ -47,7 +50,7 @@ def tile_attend_tab_timestable_exchange_kernel(
         note_pool = [keep.tile([P, U], F32, name="note_pool%d" % t) for t in range(PACK)]
         given_pool = [keep.tile([P, Z], F32, name="given_pool%d" % t) for t in range(PACK)]
         val_pool = [
-            keep.tile([P, T], F32, name="val_pool%d" % b, tag="val_pool%d" % b, align_bytes=64)
+            values.tile([P, T], F32, name="val_pool%d" % b, offset=b * POOL_BYTES)
             for b in range(E // P)
         ]
         identity = keep.tile([P, P], F32, name="identity")
@@ -170,8 +173,8 @@ def tile_attend_tab_timestable_exchange_kernel(
             return turned
 
         def multiply(b, turned):
-            val_woven = keep.tile(
-                [P, P, PACK], BF16, name="val_woven%d" % b, tag="val_pool%d" % (b + 1), align_bytes=64
+            val_woven = values.tile(
+                [P, P, PACK], BF16, name="val_woven%d" % b, offset=(b + 1) * POOL_BYTES, align_bytes=64
             )
             nc.scalar.copy(
                 val_woven[:].rearrange("p e t -> p (e t)").bitcast(F32).rearrange("p (e u) -> p e u", u=2),
@@ -187,7 +190,7 @@ def tile_attend_tab_timestable_exchange_kernel(
             return val_codes, val_scales
 
         def finish(b, val_codes, val_scales):
-            result = keep.tile([P, J], F32, name="result%d" % b, tag=("val_pool%d" % (b + 2)) if b < 2 else "result%d" % b, align_bytes=64)
+            result = values.tile([P, J], F32, name="result%d" % b, offset=(b + 2) * POOL_BYTES + WOVEN_BYTES)
             copy_out = [
                 [nc.vector.tensor_copy],
                 [nc.vector.tensor_copy],
@@ -208,7 +211,8 @@ def tile_attend_tab_timestable_exchange_kernel(
                     stop=True,
                 )
                 copy(result[:, cols], sums[:])
-            nc.sync.dma_start(out[b * P : (b + 1) * P, :], result[:])
+                queue = nc.scalar if (b == 3 and h == 0) else nc.sync
+                queue.dma_start(out[b * P : (b + 1) * P, cols], result[:, cols])
 
         turned_blocks = []
         operands = []

@@ -18,17 +18,47 @@ COPY = mybir.ActivationFunctionType.Copy
 
 P = 128
 PACK = 4
-LIST_COLS = 32
-HALF = 256
-SHARE = 176
+QUADRANT = 32
+SCALE_ROWS = 4
+LIST_COLS = I // 16
+BLOCKS = E // P
+LAST = BLOCKS - 1
+RUN = 4
+SCALAR_ALONE = 2
+SUM_BANKS = 6
+TURN_BANKS = 2
 POOL_BYTES = 4 * T
 WOVEN_BYTES = 2 * PACK * P
 
 
-def interleave(nc, woven, planes):
+def weave(nc, woven, planes):
     nc.vector.tensor_copy(
-        out=woven[:].rearrange("p (c i) t -> p c t i", i=4),
-        in_=planes[:].rearrange("p t (c i) -> p c t i", i=4),
+        out=woven[:].rearrange("p (c i) t -> p c t i", i=RUN),
+        in_=planes[:].rearrange("p t (c i) -> p c t i", i=RUN),
+    )
+
+
+def quantise(nc, pool, name, woven):
+    columns = woven.shape[1]
+    codes = pool.tile([P, columns], U32, name=name + "_codes", align_bytes=64)
+    scales = pool.tile([P, columns], U8, name=name + "_scales", align_bytes=64)
+    nc.vector.quantize_mx(
+        out=codes[:].bitcast(FP8X4),
+        scales=scales[:],
+        in_=woven[:].rearrange("p c t -> p (c t)"),
+    )
+    return codes, scales
+
+
+def product(nc, sums, lhs_codes, lhs_scales, rhs_codes, rhs_scales):
+    nc.tensor.matmul_mx(
+        out=sums,
+        lhsT=lhs_codes.bitcast(FP8X4),
+        lhsT_scale=lhs_scales,
+        rhs=rhs_codes.bitcast(FP8X4),
+        rhs_scale=rhs_scales,
+        start=True,
+        stop=True,
     )
 
 
@@ -51,7 +81,7 @@ def tile_attend_tab_timestable_exchange_kernel(
         given_pool = [keep.tile([P, Z], F32, name="given_pool%d" % t) for t in range(PACK)]
         val_pool = [
             values.tile([P, T], F32, name="val_pool%d" % b, offset=b * POOL_BYTES)
-            for b in range(E // P)
+            for b in range(BLOCKS)
         ]
         identity = keep.tile([P, P], F32, name="identity")
 
@@ -61,10 +91,13 @@ def tile_attend_tab_timestable_exchange_kernel(
         byte_rows = keep.tile([P, T // 4], I32, name="byte_rows")
         nc.sync.dma_start(note_pool[0][:], notes_by_place[0])
         nc.sync.dma_start(note_list[:], offs2)
-        for r in range(4):
-            nc.sync.dma_start(byte_rows[r:P:32, :], keys_scales[0, r:16:4, :].bitcast(I32))
-        for t in range(1, 3):
-            nc.sync.dma_start(note_pool[t][:], notes_by_place[t])
+        for r in range(SCALE_ROWS):
+            nc.sync.dma_start(
+                byte_rows[r:P:QUADRANT, :],
+                keys_scales[0, r : D // 32 : SCALE_ROWS, :].bitcast(I32),
+            )
+        nc.sync.dma_start(note_pool[1][:], notes_by_place[1])
+        nc.sync.dma_start(note_pool[2][:], notes_by_place[2])
         nc.sync.dma_start(token_list[:], offs)
         nc.sync.dma_start(note_pool[3][:], notes_by_place[3])
         nc.sync.dma_start(
@@ -76,13 +109,13 @@ def tile_attend_tab_timestable_exchange_kernel(
         nc.sync.dma_start(row_factor[:], rowf.rearrange("(p t) o -> p (t o)", t=PACK))
         for t in range(1, PACK):
             nc.sync.dma_start(given_pool[t][:], given_by_place[t])
-        for b in range(E // P):
+        for b in range(BLOCKS):
             nc.sync.dma_start(val_pool[b][:], vals[b * P : (b + 1) * P, :])
+
         nc.vector.memset(key_bytes[:].bitcast(I32), 0)
-        for q in range(4):
-            nc.vector.tensor_copy(
-                key_bytes[32 * q : 32 * q + 4, :].bitcast(I32), byte_rows[32 * q : 32 * q + 4, :]
-            )
+        for first in range(0, P, QUADRANT):
+            rows = slice(first, first + SCALE_ROWS)
+            nc.vector.tensor_copy(key_bytes[rows, :].bitcast(I32), byte_rows[rows, :])
         make_identity(nc, identity[:])
 
         note_planes = keep.tile([P, PACK, J], BF16, name="note_planes", tag="note_planes", align_bytes=64)
@@ -97,129 +130,89 @@ def tile_attend_tab_timestable_exchange_kernel(
                 nc.vector.tensor_copy(
                     key_scales[:].rearrange("p t m -> p m t"), key_bytes[:].indirect(token_list[:])
                 )
-
-        note_woven = keep.tile([P, J, PACK], BF16, name="note_woven", tag="odd_given", align_bytes=64)
-        interleave(nc, note_woven, note_planes)
+        note_woven = keep.tile([P, J, PACK], BF16, name="note_woven", align_bytes=64)
+        weave(nc, note_woven, note_planes)
         key_codes = keep.tile([P, PACK, P], U32, name="key_codes", tag="note_planes", align_bytes=64)
         nc.vector.tensor_copy(
             key_codes[:].rearrange("p t m -> p m t"), key_words[:].indirect(token_list[:])
         )
-        note_codes = keep.tile([P, J], U32, name="note_codes", align_bytes=64)
-        note_scales = keep.tile([P, J], U8, name="note_scales", align_bytes=64)
-        nc.vector.quantize_mx(
-            out=note_codes[:].bitcast(FP8X4),
-            scales=note_scales[:],
-            in_=note_woven[:].rearrange("p j t -> p (j t)"),
-        )
+        note_codes, note_scales = quantise(nc, keep, "note", note_woven)
 
-        table_planes = keep.tile([P, PACK, J], BF16, name="table_planes", tag="table_planes", align_bytes=64)
+        table_planes = keep.tile([P, PACK, J], BF16, name="table_planes", align_bytes=64)
         for t in range(PACK):
-            given_picked = keep.tile(
-                [P, J], F32, name="given_picked%d" % t,
-                tag="given_picked%d" % t, align_bytes=64,
-            )
-            picked = given_pool[t][:].indirect(given_list[:])
-            nc.scalar.activation(given_picked[:], picked, COPY)
-            products = psum.tile([P, J], F32, name="products", tag="acc", bufs=6)
-            nc.tensor.matmul_mx(
-                out=products[:],
-                lhsT=key_codes[:, t, :].bitcast(FP8X4),
-                lhsT_scale=key_scales[:, t, :],
-                rhs=note_codes[:].bitcast(FP8X4),
-                rhs_scale=note_scales[:],
-                start=True,
-                stop=True,
-            )
+            given_picked = keep.tile([P, J], F32, name="given_picked%d" % t, align_bytes=64)
+            nc.scalar.activation(given_picked[:], given_pool[t][:].indirect(given_list[:]), COPY)
+            g1 = psum.tile([P, J], F32, name="g1", tag="sums", bufs=SUM_BANKS)
+            product(nc, g1[:], key_codes[:, t, :], key_scales[:, t, :], note_codes[:], note_scales[:])
             nc.vector.scalar_tensor_tensor(
                 out=table_planes[:, t, :],
-                in0=products[:],
+                in0=g1[:],
                 scalar=row_factor[:, t : t + 1],
                 in1=given_picked[:],
                 op0=MULT,
                 op1=MULT,
             )
-        table_woven = keep.tile([P, J, PACK], BF16, name="table_woven", tag="table_woven", align_bytes=64)
-        nc.scalar.copy(
-            table_woven[:, 0:SHARE, :].rearrange("p (c i) t -> p c t i", i=4),
-            table_planes[:, :, 0:SHARE].rearrange("p t (c i) -> p c t i", i=4),
-        )
-        nc.vector.tensor_copy(
-            table_woven[:, SHARE:J, :].rearrange("p (c i) t -> p c t i", i=4),
-            table_planes[:, :, SHARE:J].rearrange("p t (c i) -> p c t i", i=4),
-        )
-        table_codes = keep.tile([P, J], U32, name="table_codes", align_bytes=64)
-        table_scales = keep.tile([P, J], U8, name="table_scales", align_bytes=64)
-        nc.vector.quantize_mx(
-            out=table_codes[:].bitcast(FP8X4),
-            scales=table_scales[:],
-            in_=table_woven[:].rearrange("p j t -> p (j t)"),
-        )
-
-        blocks = E // P
+        table_woven = keep.tile([P, J, PACK], BF16, name="table_woven", align_bytes=64)
+        weave(nc, table_woven, table_planes)
+        table_codes, table_scales = quantise(nc, keep, "table", table_woven)
 
         def gather_and_turn(b):
-            tenant_of = ["given_picked3", "table_planes", "val_picked2", "val_picked3"][b]
-            val_picked = keep.tile([P, I], BF16, name="val_picked%d" % b, tag=tenant_of, align_bytes=64)
-            nc.vector.tensor_copy(
-                val_picked[:, 0:HALF], val_pool[b][:].indirect(token_list[:, 0:16])
-            )
-            nc.scalar.activation(
-                val_picked[:, HALF:I], val_pool[b][:].indirect(token_list[:, 16:32]), COPY
-            )
+            val_picked = keep.tile([P, I], BF16, name="val_picked%d" % b)
+            if b < SCALAR_ALONE:
+                nc.scalar.activation(val_picked[:], val_pool[b][:].indirect(token_list[:]), COPY)
+            else:
+                nc.vector.tensor_copy(
+                    val_picked[:, : I // 2],
+                    val_pool[b][:].indirect(token_list[:, : LIST_COLS // 2]),
+                )
+                nc.scalar.activation(
+                    val_picked[:, I // 2 :],
+                    val_pool[b][:].indirect(token_list[:, LIST_COLS // 2 :]),
+                    COPY,
+                )
             pairs = val_picked[:].bitcast(F32)
-            turned = psum.tile([P, 2, P], F32, name="turned", tag="turned", bufs=2)
+            turned = psum.tile([P, 2, P], F32, name="turned", tag="turned", bufs=TURN_BANKS)
             for u in range(2):
-                nc.tensor.transpose(turned[:, u, :], pairs[:, u : 2 * P : 2], identity[:])
+                nc.tensor.transpose(turned[:, u, :], pairs[:, u : I // 2 : 2], identity[:])
             return turned
 
-        def multiply(b, turned):
+        def weave_and_quantise(b, turned):
+            place = b + 1 if b > 0 else b
             val_woven = values.tile(
-                [P, P, PACK], BF16, name="val_woven%d" % b, offset=(b + 1) * POOL_BYTES, align_bytes=64
+                [P, P, PACK], BF16, name="val_woven%d" % b, offset=place * POOL_BYTES, align_bytes=64
             )
+            woven_words = val_woven[:].rearrange("p e t -> p (e t)").bitcast(F32)
             nc.scalar.copy(
-                val_woven[:].rearrange("p e t -> p (e t)").bitcast(F32).rearrange("p (e u) -> p e u", u=2),
-                turned[:].rearrange("p u e -> p e u"),
+                woven_words.rearrange("p (e u) -> p e u", u=2), turned[:].rearrange("p u e -> p e u")
             )
-            val_codes = keep.tile([P, P], U32, name="val_codes%d" % b, align_bytes=64)
-            val_scales = keep.tile([P, P], U8, name="val_scales%d" % b, align_bytes=64)
-            nc.vector.quantize_mx(
-                out=val_codes[:].bitcast(FP8X4),
-                scales=val_scales[:],
-                in_=val_woven[:].rearrange("p e t -> p (e t)"),
-            )
-            return val_codes, val_scales
+            return quantise(nc, keep, "val%d" % b, val_woven)
 
-        def finish(b, val_codes, val_scales):
-            result = values.tile([P, J], F32, name="result%d" % b, offset=(b + 2) * POOL_BYTES + WOVEN_BYTES)
-            copy_out = [
-                [nc.vector.tensor_copy],
-                [nc.vector.tensor_copy],
-                [nc.scalar.copy],
-                [nc.scalar.copy, nc.vector.tensor_copy],
-            ][b]
-            width = J // len(copy_out)
-            for h, copy in enumerate(copy_out):
-                cols = slice(h * width, (h + 1) * width)
-                sums = psum.tile([P, width], F32, name="sums", tag="acc", bufs=6)
-                nc.tensor.matmul_mx(
-                    out=sums[:],
-                    lhsT=val_codes[:].bitcast(FP8X4),
-                    lhsT_scale=val_scales[:],
-                    rhs=table_codes[:, cols].bitcast(FP8X4),
-                    rhs_scale=table_scales[:, cols],
-                    start=True,
-                    stop=True,
-                )
-                copy(result[:, cols], sums[:])
-                queue = nc.scalar if (b == 3 and h == 0) else nc.sync
-                queue.dma_start(out[b * P : (b + 1) * P, cols], result[:, cols])
+        def multiply_and_store(b, val_codes, val_scales):
+            result = values.tile(
+                [P, J], F32, name="result%d" % b, offset=(b + 2) * POOL_BYTES + WOVEN_BYTES
+            )
+            if b == LAST:
+                copies = [nc.scalar.copy, nc.vector.tensor_copy]
+            elif b == LAST - 1:
+                copies = [nc.scalar.copy]
+            else:
+                copies = [nc.vector.tensor_copy]
+            width = J // len(copies)
+            for n, copy_out in enumerate(copies):
+                cols = slice(n * width, (n + 1) * width)
+                sums = psum.tile([P, width], F32, name="sums", tag="sums", bufs=SUM_BANKS)
+                product(nc, sums[:], val_codes[:], val_scales[:], table_codes[:, cols], table_scales[:, cols])
+                copy_out(result[:, cols], sums[:])
+            nc.sync.dma_start(out[b * P : (b + 1) * P, :], result[:])
 
         turned_blocks = []
         operands = []
-        for step in range(blocks + 2):
-            if step < blocks:
+        for step in range(BLOCKS + 2):
+            if step < BLOCKS:
                 turned_blocks.append(gather_and_turn(step))
-            if 1 <= step <= blocks:
-                operands.append(multiply(step - 1, turned_blocks[step - 1]))
+            if step == 0:
+                operands.append(weave_and_quantise(0, turned_blocks[0]))
+            if 2 <= step <= BLOCKS:
+                operands.append(weave_and_quantise(step - 1, turned_blocks[step - 1]))
             if step >= 2:
-                finish(step - 2, *operands[step - 2])
+                multiply_and_store(step - 2, *operands[step - 2])

from contextlib import ExitStack

import concourse.mybir as mybir
from concourse.masks import make_identity

D, T, I, J, U, Z, E = 512, 2048, 512, 512, 1024, 1024, 512
FLOPS = 2 * D * I * J + 2 * I * E * J

F32 = mybir.dt.float32
BF16 = mybir.dt.bfloat16
I32 = mybir.dt.int32
U32 = mybir.dt.uint32
U16 = mybir.dt.uint16
U8 = mybir.dt.uint8
FP8X4 = mybir.dt.float8_e4m3fn_x4
MULT = mybir.AluOpType.mult
COPY = mybir.ActivationFunctionType.Copy

P = 128
PACK = 4
QUADRANT = 32
SCALE_ROWS = 4
LIST_COLS = I // 16
BLOCKS = E // P
LAST = BLOCKS - 1
RUN = 4
SCALAR_ALONE = 2
SUM_BANKS = 6
TURN_BANKS = 2
POOL_BYTES = 4 * T
WOVEN_BYTES = 2 * PACK * P


def weave(nc, woven, planes):
    nc.vector.tensor_copy(
        out=woven[:].rearrange("p (c i) t -> p c t i", i=RUN),
        in_=planes[:].rearrange("p t (c i) -> p c t i", i=RUN),
    )


def quantise(nc, pool, name, woven):
    columns = woven.shape[1]
    codes = pool.tile([P, columns], U32, name=name + "_codes", align_bytes=64)
    scales = pool.tile([P, columns], U8, name=name + "_scales", align_bytes=64)
    nc.vector.quantize_mx(
        out=codes[:].bitcast(FP8X4),
        scales=scales[:],
        in_=woven[:].rearrange("p c t -> p (c t)"),
    )
    return codes, scales


def product(nc, sums, lhs_codes, lhs_scales, rhs_codes, rhs_scales):
    nc.tensor.matmul_mx(
        out=sums,
        lhsT=lhs_codes.bitcast(FP8X4),
        lhsT_scale=lhs_scales,
        rhs=rhs_codes.bitcast(FP8X4),
        rhs_scale=rhs_scales,
        start=True,
        stop=True,
    )


def tile_attend_tab_timestable_exchange_kernel(
    tc, keys_words, keys_scales, notes, given, rowf, vals, offs, offs2, offs3, out
):
    nc = tc.nc
    with ExitStack() as ctx:
        keep = ctx.enter_context(tc.tile_pool(name="keep", bufs=1))
        values = ctx.enter_context(tc.tile_pool(name="values", bufs=1))
        psum = ctx.enter_context(tc.psum_pool(name="psum", bufs=1))

        token_list = keep.tile([P, LIST_COLS], U16, name="token_list")
        note_list = keep.tile([P, LIST_COLS], U16, name="note_list")
        given_list = keep.tile([P, LIST_COLS], U16, name="given_list")
        key_words = keep.tile([P, T], U32, name="key_words")
        key_bytes = keep.tile([P, T], U8, name="key_bytes")
        row_factor = keep.tile([P, PACK], F32, name="row_factor")
        note_pool = [keep.tile([P, U], F32, name="note_pool%d" % t) for t in range(PACK)]
        given_pool = [keep.tile([P, Z], F32, name="given_pool%d" % t) for t in range(PACK)]
        val_pool = [
            values.tile([P, T], F32, name="val_pool%d" % b, offset=b * POOL_BYTES)
            for b in range(BLOCKS)
        ]
        identity = keep.tile([P, P], F32, name="identity")

        notes_by_place = notes.rearrange("(p t) u -> t p u", t=PACK)
        given_by_place = given.rearrange("(p t) z -> t p z", t=PACK)

        byte_rows = keep.tile([P, T // 4], I32, name="byte_rows")
        nc.sync.dma_start(note_pool[0][:], notes_by_place[0])
        nc.sync.dma_start(note_list[:], offs2)
        for r in range(SCALE_ROWS):
            nc.sync.dma_start(
                byte_rows[r:P:QUADRANT, :],
                keys_scales[0, r : D // 32 : SCALE_ROWS, :].bitcast(I32),
            )
        nc.sync.dma_start(note_pool[1][:], notes_by_place[1])
        nc.sync.dma_start(note_pool[2][:], notes_by_place[2])
        nc.sync.dma_start(token_list[:], offs)
        nc.sync.dma_start(note_pool[3][:], notes_by_place[3])
        nc.sync.dma_start(
            key_words[:].bitcast(I32),
            keys_words[0].rearrange("p n t -> p (n t)").bitcast(I32),
        )
        nc.sync.dma_start(given_list[:], offs3)
        nc.sync.dma_start(given_pool[0][:], given_by_place[0])
        nc.sync.dma_start(row_factor[:], rowf.rearrange("(p t) o -> p (t o)", t=PACK))
        for t in range(1, PACK):
            nc.sync.dma_start(given_pool[t][:], given_by_place[t])
        for b in range(BLOCKS):
            nc.sync.dma_start(val_pool[b][:], vals[b * P : (b + 1) * P, :])

        nc.vector.memset(key_bytes[:].bitcast(I32), 0)
        for first in range(0, P, QUADRANT):
            rows = slice(first, first + SCALE_ROWS)
            nc.vector.tensor_copy(key_bytes[rows, :].bitcast(I32), byte_rows[rows, :])
        make_identity(nc, identity[:])

        note_planes = keep.tile([P, PACK, J], BF16, name="note_planes", tag="note_planes", align_bytes=64)
        key_scales = keep.tile([P, PACK, P], U8, name="key_scales", align_bytes=64)
        for t in range(PACK):
            picked = note_pool[t][:].indirect(note_list[:])
            if t % 2 == 0:
                nc.scalar.activation(note_planes[:, t, :], picked, COPY)
            else:
                nc.vector.tensor_copy(note_planes[:, t, :], picked)
            if t == 1:
                nc.vector.tensor_copy(
                    key_scales[:].rearrange("p t m -> p m t"), key_bytes[:].indirect(token_list[:])
                )
        note_woven = keep.tile([P, J, PACK], BF16, name="note_woven", align_bytes=64)
        weave(nc, note_woven, note_planes)
        key_codes = keep.tile([P, PACK, P], U32, name="key_codes", tag="note_planes", align_bytes=64)
        nc.vector.tensor_copy(
            key_codes[:].rearrange("p t m -> p m t"), key_words[:].indirect(token_list[:])
        )
        note_codes, note_scales = quantise(nc, keep, "note", note_woven)

        table_planes = keep.tile([P, PACK, J], BF16, name="table_planes", align_bytes=64)
        for t in range(PACK):
            given_picked = keep.tile([P, J], F32, name="given_picked%d" % t, align_bytes=64)
            nc.scalar.activation(given_picked[:], given_pool[t][:].indirect(given_list[:]), COPY)
            g1 = psum.tile([P, J], F32, name="g1", tag="sums", bufs=SUM_BANKS)
            product(nc, g1[:], key_codes[:, t, :], key_scales[:, t, :], note_codes[:], note_scales[:])
            nc.vector.scalar_tensor_tensor(
                out=table_planes[:, t, :],
                in0=g1[:],
                scalar=row_factor[:, t : t + 1],
                in1=given_picked[:],
                op0=MULT,
                op1=MULT,
            )
        table_woven = keep.tile([P, J, PACK], BF16, name="table_woven", align_bytes=64)
        weave(nc, table_woven, table_planes)
        table_codes, table_scales = quantise(nc, keep, "table", table_woven)

        def gather_and_turn(b):
            val_picked = keep.tile([P, I], BF16, name="val_picked%d" % b)
            if b < SCALAR_ALONE:
                nc.scalar.activation(val_picked[:], val_pool[b][:].indirect(token_list[:]), COPY)
            else:
                nc.vector.tensor_copy(
                    val_picked[:, : I // 2],
                    val_pool[b][:].indirect(token_list[:, : LIST_COLS // 2]),
                )
                nc.scalar.activation(
                    val_picked[:, I // 2 :],
                    val_pool[b][:].indirect(token_list[:, LIST_COLS // 2 :]),
                    COPY,
                )
            pairs = val_picked[:].bitcast(F32)
            turned = psum.tile([P, 2, P], F32, name="turned", tag="turned", bufs=TURN_BANKS)
            for u in range(2):
                nc.tensor.transpose(turned[:, u, :], pairs[:, u : I // 2 : 2], identity[:])
            return turned

        def weave_and_quantise(b, turned):
            place = b + 1 if b > 0 else b
            val_woven = values.tile(
                [P, P, PACK], BF16, name="val_woven%d" % b, offset=place * POOL_BYTES, align_bytes=64
            )
            woven_words = val_woven[:].rearrange("p e t -> p (e t)").bitcast(F32)
            nc.scalar.copy(
                woven_words.rearrange("p (e u) -> p e u", u=2), turned[:].rearrange("p u e -> p e u")
            )
            return quantise(nc, keep, "val%d" % b, val_woven)

        def multiply_and_store(b, val_codes, val_scales):
            result = values.tile(
                [P, J], F32, name="result%d" % b, offset=(b + 2) * POOL_BYTES + WOVEN_BYTES
            )
            if b == LAST:
                copies = [nc.scalar.copy, nc.vector.tensor_copy]
            elif b == LAST - 1:
                copies = [nc.scalar.copy]
            else:
                copies = [nc.vector.tensor_copy]
            width = J // len(copies)
            for n, copy_out in enumerate(copies):
                cols = slice(n * width, (n + 1) * width)
                sums = psum.tile([P, width], F32, name="sums", tag="sums", bufs=SUM_BANKS)
                product(nc, sums[:], val_codes[:], val_scales[:], table_codes[:, cols], table_scales[:, cols])
                copy_out(result[:, cols], sums[:])
            nc.sync.dma_start(out[b * P : (b + 1) * P, :], result[:])

        turned_blocks = []
        operands = []
        for step in range(BLOCKS + 2):
            if step < BLOCKS:
                turned_blocks.append(gather_and_turn(step))
            if step == 0:
                operands.append(weave_and_quantise(0, turned_blocks[0]))
            if 2 <= step <= BLOCKS:
                operands.append(weave_and_quantise(step - 1, turned_blocks[step - 1]))
            if step >= 2:
                multiply_and_store(step - 2, *operands[step - 2])
